import numpy as np
import ml_dtypes


def mxq(x, axis, fmt="e4m3"):
    dtype, down = {"e4m3": (ml_dtypes.float8_e4m3fn, 7), "e5m2": (ml_dtypes.float8_e5m2, 14)}[fmt]
    v = np.moveaxis(np.asarray(x, np.float32).astype(ml_dtypes.bfloat16).astype(np.float64), axis, -1)
    blocks = v.reshape(v.shape[:-1] + (-1, 32))
    amax = np.abs(blocks).max(-1, keepdims=True)
    byte = np.maximum(np.where(amax > 0, np.frexp(amax)[1] - 1 + 127, 0) - down, 1)
    scale = np.exp2(byte - 127.0)
    codes = (blocks / scale).astype(np.float32).astype(dtype).astype(np.float64)
    return np.moveaxis((codes * scale).reshape(v.shape), -1, axis)


WIDE = False


def mx_kscale(k):
    if not WIDE:
        return np.ones(k)
    levels = np.array([30, -30])
    if k % 512:
        return np.exp2(np.random.permutation(np.resize(levels, k // 32))).repeat(32)
    a = np.empty((k // 512, 16))
    for p in range(k // 512):
        a[p, :8] = np.random.permutation(np.resize(levels, 8))
        for g in range(8):
            far = levels[np.abs(levels - a[p, g]) >= 10]
            a[p, g + 8] = far[np.random.randint(len(far))]
    return np.exp2(a.ravel()).repeat(32)


def f64(x):
    return np.asarray(x).astype(np.float64)


def striped(idx):
    return np.tile(np.asarray(idx).reshape(-1, 16).T, (8, 1)).astype(np.uint16)


def unstriped(offs):
    return offs[:16].T.reshape(-1).astype(np.int64)


E2M1 = np.array([0.0, 0.5, 1.0, 1.5, 2.0, 3.0, 4.0, 6.0, -0.0, -0.5, -1.0, -1.5, -2.0, -3.0, -4.0, -6.0])


def pack_weight(w, fmt):
    k, n = w.shape
    w = f64(np.asarray(w, np.float32).astype(ml_dtypes.bfloat16)).reshape(k // 32, 32, n)
    amax = np.abs(w).max(1)
    if fmt in ("e4m3", "e5m2"):
        byte = np.frexp(amax)[1] - 1 + 127 - (7 if fmt == "e4m3" else 14)
    else:
        mant, ex = np.frexp(amax / 6.0)
        byte = np.where(mant > 0.5, ex, ex - 1) + 127
    byte = np.clip(np.where(amax > 0, byte, 1), 1, 254)
    scaled = (w * np.exp2(127.0 - byte)[:, None, :]).reshape(k, n).astype(np.float32)
    by_word = np.ascontiguousarray(scaled.reshape(k // 512, 128, 4, n).transpose(0, 1, 3, 2))
    if fmt in ("e4m3", "e5m2"):
        words = by_word.astype(ml_dtypes.float8_e4m3fn if fmt == "e4m3" else ml_dtypes.float8_e5m2).view(np.uint8)
    else:
        c = by_word.astype(ml_dtypes.float4_e2m1fn).view(np.uint8) & 0xF
        words = (c[..., 0::2] | (c[..., 1::2] << 4)).reshape(k // 512, 128, 2 * n)
    return np.ascontiguousarray(words), np.ascontiguousarray(byte.astype(np.uint8).reshape(k // 512, 16, n))


def unpack_weight(words, scales, fmt):
    g, _, n = scales.shape
    words = np.ascontiguousarray(words).reshape(g, 128, n, -1)
    if fmt in ("e4m3", "e5m2"):
        vals = words.view(ml_dtypes.float8_e4m3fn if fmt == "e4m3" else ml_dtypes.float8_e5m2).astype(np.float64)
    else:
        nib = np.empty((g, 128, n, 4), np.uint8)
        nib[..., 0::2] = words & 0xF
        nib[..., 1::2] = words >> 4
        vals = E2M1[nib]
    vals = vals * np.repeat(np.exp2(scales.astype(np.float64) - 127.0), 8, axis=1)[..., None]
    return vals.transpose(0, 1, 3, 2).reshape(g * 512, n)


def bf(x):
    return np.asarray(x, np.float32).astype(ml_dtypes.bfloat16)


def planes(Y):
    r, m = Y.shape
    b = f64(bf(Y)).reshape(r // 32, 32, m)
    amax = np.abs(b).max(1)
    byte = np.clip(np.where(amax > 0, np.frexp(amax)[1] - 1 + 127 - 7, 1), 1, 254)
    codes = (b * np.exp2(127.0 - byte)[:, None, :]).reshape(r, m).astype(np.float32).astype(ml_dtypes.float8_e4m3fn).view(np.uint8)
    words = codes.reshape(r // 512, 128, 4, m).transpose(0, 1, 3, 2)
    return np.ascontiguousarray(words), np.ascontiguousarray(byte.astype(np.uint8).reshape(r // 512, 16, m))


K, T, J, I, L, S, R, X, N, Z = 1024, 1024, 256, 128, 128, 512, 512, 512, 512, 512


def setup_inputs():
    n = np.random.standard_normal
    idx = np.random.permutation(T)[:I]
    idx2 = np.random.permutation(S)[:L]
    idx3 = np.random.permutation(Z)[:J]
    fk = mx_kscale(K)
    fr = mx_kscale(R)
    fx = mx_kscale(X)
    wp = pack_weight(n((K, R)) * 1 / np.sqrt(K) * fk[:, None] * fr, "e5m2")
    sxp = pack_weight(n((X, J)) / fx[:, None], "e4m3")
    wsp = pack_weight(n((X, R)) * 1 / np.sqrt(X) * fx[:, None] * fr, "e4m3")
    return {
        "xa": (n((K, T)) / fk[:, None]).astype(np.float32),
        "xb": (n((K, S)) * 0.6 / fk[:, None]).astype(np.float32),
        "w_words": wp[0],
        "w_scales": wp[1],
        "sx_words": sxp[0],
        "sx_scales": sxp[1],
        "ws_words": wsp[0],
        "ws_scales": wsp[1],
        "wb": (n((R, N)) * 1 / np.sqrt(R) / fr[:, None]).astype(np.float32),
        "tz": (n((N, Z)) * 0.6).astype(np.float32),
        "rw": (np.random.uniform(0.5, 2.0, (1, J))).astype(np.float32),
        "offs": striped(idx),
        "offs2": striped(idx2),
        "offs3": striped(idx3),
    }


def reference(xa, xb, w_words, w_scales, sx_words, sx_scales, ws_words, ws_scales, wb, tz, rw, offs, offs2, offs3):
    idx = unstriped(offs)
    idx2 = unstriped(offs2)
    idx3 = unstriped(offs3)
    wu = unpack_weight(w_words, w_scales, "e5m2")
    sxu = unpack_weight(sx_words, sx_scales, "e4m3")
    wsu = unpack_weight(ws_words, ws_scales, "e4m3")
    u = np.concatenate([f64(xa)[:, idx], f64(xb)[:, idx2]], axis=1)
    uq = mxq(u, 0, "e4m3")
    a = wu.T @ uq
    b2 = wsu.T @ sxu
    hid = np.maximum(a, b2)
    wbq = mxq(f64(wb), 0, "e4m3")
    hidq = mxq(hid, 0, "e5m2")
    p = wbq.T @ hidq
    y = np.maximum(p, f64(tz)[:, idx3]) * f64(rw)
    words, scales = planes(y)
    return y, words, scales

@@ -1,0 +1,245 @@
+from contextlib import ExitStack
+
+import concourse.mybir as mybir
+from concourse.masks import make_identity
+
+F32 = mybir.dt.float32
+BF16 = mybir.dt.bfloat16
+I32 = mybir.dt.int32
+U32 = mybir.dt.uint32
+U16 = mybir.dt.uint16
+U8 = mybir.dt.uint8
+E4M3 = mybir.dt.float8_e4m3fn_x4
+E5M2 = mybir.dt.float8_e5m2_x4
+MAX = mybir.AluOpType.max
+MULT = mybir.AluOpType.mult
+COPY = mybir.ActivationFunctionType.Copy
+
+P = 128
+PACK = 4
+K_PASS = P * PACK
+K, T, S, J, R, X, N, Z = 1024, 1024, 512, 256, 512, 512, 512, 512
+HALF = J // 2
+PASSES = K // K_PASS
+
+FLOPS = 2 * J * (K * R + X * R + R * N)
+
+
+def tile_list_joined_rival_floored_pl_kernel(
+    tc, xa, xb, w_words, w_scales, sx_words, sx_scales, ws_words, ws_scales, wb, tz, rw,
+    offs, offs2, offs3, out_0, out_1, out_2,
+):
+    nc = tc.nc
+    with ExitStack() as ctx:
+        lists = ctx.enter_context(tc.tile_pool(name="lists", bufs=1))
+        sb = ctx.enter_context(tc.tile_pool(name="sb", bufs=1))
+        psum = ctx.enter_context(tc.psum_pool(name="psum", bufs=1))
+
+        def tile(name, shape, dtype):
+            return sb.tile(shape, dtype, name=name, align_bytes=64)
+
+        def load_rows(name, table, first_row, slots):
+            width = table.shape[1]
+            rows = table[first_row : first_row + K_PASS, :].rearrange("(p t) c -> p t c", t=PACK)
+            held = tile(name, [P, len(slots) * width], F32)
+            nc.sync.dma_start(
+                out=held[:].rearrange("p (t c) -> p t c", c=width), in_=rows[:, slots[0] : slots[-1] + 1, :]
+            )
+            return [held[:, i * width : (i + 1) * width] for i in range(len(slots))]
+
+        def load_list(name, source):
+            held = lists.tile(list(source.shape), U16, name=name)
+            nc.sync.dma_start(held[:], source)
+            return held
+
+        def load_words(name, words):
+            passes, width = words.shape[0], words.shape[2]
+            held = tile(name, [P, passes * width], U32)
+            nc.sync.dma_start(
+                out=held[:].bitcast(I32).rearrange("p (z c) -> p z c", z=passes),
+                in_=words.rearrange("z p c t -> p z (c t)").bitcast(I32),
+            )
+            return held
+
+        def load_scale_rows(queue, held, scales, q):
+            queue.dma_start(
+                out=held[32 * q : 32 * q + 4, :].bitcast(I32).rearrange("p (z c) -> p z c", z=scales.shape[0]),
+                in_=scales[:, 4 * q : 4 * q + 4, :].rearrange("z r c -> r z c").bitcast(I32),
+            )
+
+        def deal(name, held, dtype):
+            passes = held.shape[1] // R
+            dealt = tile(name, [P, passes * R], dtype)
+            nc.vector.tensor_copy(
+                out=dealt[:].rearrange("p (z t m) -> p z m t", t=PACK, m=P),
+                in_=held[:].rearrange("p (z m t) -> p z m t", t=PACK, m=P),
+            )
+            return dealt
+
+        def quantise(name, grouped, fmt):
+            width = grouped.shape[1] // PACK
+            codes = tile(name + "_codes", [P, width], U32)
+            scales = tile(name + "_scales", [P, width], U8)
+            nc.vector.quantize_mx(out=codes[:].bitcast(fmt), scales=scales[:], in_=grouped[:])
+            return codes, scales
+
+        landed = tile("landed", [P, (PASSES + 1) * R], U8)
+        w_rows, ws_rows = landed[:, : PASSES * R], landed[:, PASSES * R :]
+        xb_planes = load_rows("xb0", xb, 0, [0, 1, 2, 3])
+        list_b = load_list("list_b", offs2)
+        load_scale_rows(nc.sync, w_rows, w_scales, 0)
+        load_scale_rows(nc.sync, w_rows, w_scales, 1)
+        xb_planes = xb_planes + load_rows("xb1", xb, K_PASS, [0, 1, 2, 3])
+        load_scale_rows(nc.sync, w_rows, w_scales, 2)
+        load_scale_rows(nc.sync, w_rows, w_scales, 3)
+        list_a = load_list("list_a", offs)
+        w_raw = load_words("w_raw", w_words)
+        ws_raw = load_words("ws_raw", ws_words)
+        sx_codes = load_words("sx_codes", sx_words)
+        load_scale_rows(nc.sync, ws_rows, ws_scales, 0)
+        wb_raw = tile("wb_raw", [P, PACK * N], F32)
+        nc.sync.dma_start(out=wb_raw[:], in_=wb.rearrange("(p i) n -> p (i n)", i=PACK))
+        for q in range(1, 4):
+            load_scale_rows(nc.sync, ws_rows, ws_scales, q)
+        xa_planes = load_rows("xa0", xa, 0, [0, 1])
+        list_z = load_list("list_z", offs3)
+        for name, first_row, slots in (
+            ("xa1", 0, [2, 3]), ("xa2", K_PASS, [0, 1]), ("xa3", K_PASS, [2]), ("xa4", K_PASS, [3])
+        ):
+            xa_planes = xa_planes + load_rows(name, xa, first_row, slots)
+        tz_planes = [load_rows("tz%d" % t, tz, 0, [t])[0] for t in range(PACK)]
+
+        sx_scale = tile("sx_scale", [P, J], U8)
+        nc.gpsimd.memset(sx_scale[:].bitcast(I32), 0)
+        for q in range(4):
+            load_scale_rows(nc.gpsimd, sx_scale, sx_scales, q)
+        rw_cols = tile("rw_cols", [P, 2], F32)
+        nc.gpsimd.dma_start(out=rw_cols[:], in_=rw.rearrange("o (p e) -> (o p) e", e=2))
+
+        filled = tile("filled", [P, (PASSES + 1) * R], U8)
+        nc.vector.memset(filled[:].bitcast(I32), 0)
+
+        identity = tile("identity", [P, P], F32)
+        make_identity(nc, identity[:])
+        rw_bank = psum.tile([P, 2, P], F32, name="rw_bank")
+        for e in range(2):
+            nc.tensor.transpose(rw_bank[:, e, :], rw_cols[:, e : e + 1].to_broadcast([P, P]), identity[:])
+        rw_rows = tile("rw_rows", [P, J], F32)
+        nc.scalar.copy(out=rw_rows[:].rearrange("p (n e) -> p n e", e=2), in_=rw_bank[:].rearrange("p e n -> p n e"))
+
+        def gather_pass(h, z, planes, offsets):
+            grouped = tile("u%d%d" % (h, z), [P, HALF * PACK], BF16)
+            slots = grouped[:].rearrange("p (j t) -> p j t", t=PACK)
+            for t in range(PACK):
+                nc.vector.tensor_copy(out=slots[:, :, t], in_=planes[PACK * z + t].indirect(offsets[:]))
+            return quantise("u%d%d" % (h, z), grouped, E4M3)
+
+        u_b = [gather_pass(1, z, xb_planes, list_b) for z in range(PASSES)]
+
+        w_codes = deal("w_codes", w_raw, U32)
+        ws_codes = deal("ws_codes", ws_raw, U32)
+        for q in range(4):
+            live = slice(32 * q, 32 * q + 4)
+            nc.vector.tensor_copy(out=filled[live, :].bitcast(I32), in_=landed[live, :].bitcast(I32))
+        dealt_scales = deal("dealt_scales", filled, U8)
+        w_scale, ws_scale = dealt_scales[:, : PASSES * R], dealt_scales[:, PASSES * R :]
+
+        def own_product(h):
+            bank = psum.tile([P, PACK, HALF], F32, name="b2_bank%d" % h)
+            cols = slice(h * HALF, (h + 1) * HALF)
+            for t in range(PACK):
+                rows = slice(t * P, (t + 1) * P)
+                nc.tensor.matmul_mx(
+                    out=bank[:, t, :], lhsT=ws_codes[:, rows].bitcast(E4M3), lhsT_scale=ws_scale[:, rows],
+                    rhs=sx_codes[:, cols].bitcast(E4M3), rhs_scale=sx_scale[:, cols], start=True, stop=True,
+                )
+            b2 = tile("b2_%d" % h, [P, HALF, PACK], F32)
+            nc.scalar.copy(out=b2[:], in_=bank[:].rearrange("p t j -> p j t"))
+            return b2
+
+        b2_b = own_product(1)
+        b2_a = own_product(0)
+
+        wb_grouped = tile("wb_grouped", [P, N * PACK], BF16)
+        nc.scalar.copy(
+            out=wb_grouped[:].rearrange("p (t m i) -> p m t i", t=PACK, i=PACK),
+            in_=wb_raw[:].rearrange("p (i m t) -> p m t i", t=PACK, i=PACK),
+        )
+
+        def first_pass(bank, z, u):
+            codes, scales = u
+            for t in range(PACK):
+                rows = slice(z * R + t * P, z * R + (t + 1) * P)
+                nc.tensor.matmul_mx(
+                    out=bank[:, t, :], lhsT=w_codes[:, rows].bitcast(E5M2), lhsT_scale=w_scale[:, rows],
+                    rhs=codes[:].bitcast(E4M3), rhs_scale=scales[:],
+                    start=(z == 0 and t == 0), stop=(z == PASSES - 1 and t == PACK - 1),
+                )
+
+        def hidden(h, bank, b2):
+            grouped = tile("hid%d" % h, [P, HALF * PACK], BF16)
+            nc.vector.tensor_tensor(
+                out=grouped[:].rearrange("p (j t) -> p j t", t=PACK), in0=bank[:].rearrange("p t j -> p j t"),
+                in1=b2[:], op=MAX,
+            )
+            return quantise("hid%d" % h, grouped, E5M2)
+
+        def second_product(h, hid):
+            codes, scales = hid
+            bank = psum.tile([P, PACK, HALF], F32, name="p_bank%d" % h)
+            for t in range(PACK):
+                rows = slice(t * P, (t + 1) * P)
+                nc.tensor.matmul_mx(
+                    out=bank[:, t, :], lhsT=wb_codes[:, rows].bitcast(E4M3), lhsT_scale=wb_scale[:, rows],
+                    rhs=codes[:].bitcast(E5M2), rhs_scale=scales[:], start=True, stop=True,
+                )
+            return bank
+
+        a_bank_b = psum.tile([P, PACK, HALF], F32, name="a_bank1")
+        for z in range(PASSES):
+            first_pass(a_bank_b, z, u_b[z])
+        hid_b = hidden(1, a_bank_b, b2_b)
+        wb_codes, wb_scale = quantise("wb", wb_grouped, E4M3)
+        p_b = second_product(1, hid_b)
+
+        a_bank_a = psum.tile([P, PACK, HALF], F32, name="a_bank0")
+        for z in range(PASSES):
+            first_pass(a_bank_a, z, gather_pass(0, z, xa_planes, list_a))
+        hid_a = hidden(0, a_bank_a, b2_a)
+        p_a = second_product(0, hid_a)
+
+        floors = [tile("floor%d" % h, [P, PACK, HALF], F32) for h in range(2)]
+        for t in range(PACK):
+            for h in (1, 0):
+                offsets = list_z[:, h * HALF // 16 : (h + 1) * HALF // 16]
+                nc.scalar.activation(out=floors[h][:, t, :], in_=tz_planes[t].indirect(offsets), func=COPY)
+
+        y_codes = tile("y_codes", [P, J], U32)
+        y_scales = tile("y_scales", [P, J], U8)
+        out_rows = out_0.rearrange("(p t) j -> p t j", t=PACK)
+        out_words = out_1.rearrange("z p c t -> p (z c t)").bitcast(I32)
+
+        def finish(h, bank, round_on):
+            cols = slice(h * HALF, (h + 1) * HALF)
+            floored = tile("floored%d" % h, [P, PACK, HALF], F32)
+            nc.vector.tensor_tensor(out=floored[:], in0=bank[:], in1=floors[h][:], op=MAX)
+            y = tile("y%d" % h, [P, PACK, HALF], F32)
+            nc.vector.tensor_tensor(
+                out=y[:], in0=floored[:], in1=rw_rows[:, cols].unsqueeze(1).to_broadcast([P, PACK, HALF]), op=MULT
+            )
+            nc.sync.dma_start(out=out_rows[:, :, cols], in_=y[:])
+            grouped = tile("y_grouped%d" % h, [P, HALF * PACK], BF16)
+            round_on(
+                out=grouped[:].rearrange("p (c i t) -> p c t i", t=PACK, i=4),
+                in_=y[:].rearrange("p t (c i) -> p c t i", i=4),
+            )
+            nc.vector.quantize_mx(out=y_codes[:, cols].bitcast(E4M3), scales=y_scales[:, cols], in_=grouped[:])
+            nc.sync.dma_start(out=out_words[:, cols], in_=y_codes[:, cols].bitcast(I32))
+
+        finish(1, p_b, nc.scalar.copy)
+        finish(0, p_a, nc.vector.tensor_copy)
+        for q in range(4):
+            queue = nc.scalar if q % 2 else nc.sync
+            queue.dma_start(
+                out=out_2[0, 4 * q : 4 * q + 4, :].bitcast(I32), in_=y_scales[32 * q : 32 * q + 4, :].bitcast(I32)
+            )

@@ -21,6 +21,8 @@ K_PASS = P * PACK
 K, T, S, J, R, X, N, Z = 1024, 1024, 512, 256, 512, 512, 512, 512
 HALF = J // 2
 PASSES = K // K_PASS
+PAIR = 2
+DEALT = (PASSES + 1) * R
 
 FLOPS = 2 * J * (K * R + X * R + R * N)
 
@@ -61,18 +63,18 @@ def tile_list_joined_rival_floored_pl_kernel(
             )
             return held
 
-        def load_scale_rows(queue, held, scales, q):
-            queue.dma_start(
+        def load_scale_rows(held, scales, q):
+            nc.sync.dma_start(
                 out=held[32 * q : 32 * q + 4, :].bitcast(I32).rearrange("p (z c) -> p z c", z=scales.shape[0]),
                 in_=scales[:, 4 * q : 4 * q + 4, :].rearrange("z r c -> r z c").bitcast(I32),
             )
 
-        def deal(name, held, dtype):
+        def deal(name, held, dtype, walk):
             passes = held.shape[1] // R
             dealt = tile(name, [P, passes * R], dtype)
             nc.vector.tensor_copy(
-                out=dealt[:].rearrange("p (z t m) -> p z m t", t=PACK, m=P),
-                in_=held[:].rearrange("p (z m t) -> p z m t", t=PACK, m=P),
+                out=dealt[:].rearrange("p (z t m) -> " + walk, t=PACK, m=P),
+                in_=held.rearrange("p (z m t) -> " + walk, t=PACK, m=P),
             )
             return dealt
 
@@ -83,40 +85,33 @@ def tile_list_joined_rival_floored_pl_kernel(
             nc.vector.quantize_mx(out=codes[:].bitcast(fmt), scales=scales[:], in_=grouped[:])
             return codes, scales
 
-        landed = tile("landed", [P, (PASSES + 1) * R], U8)
-        w_rows, ws_rows = landed[:, : PASSES * R], landed[:, PASSES * R :]
-        xb_planes = load_rows("xb0", xb, 0, [0, 1, 2, 3])
-        list_b = load_list("list_b", offs2)
-        load_scale_rows(nc.sync, w_rows, w_scales, 0)
-        load_scale_rows(nc.sync, w_rows, w_scales, 1)
-        xb_planes = xb_planes + load_rows("xb1", xb, K_PASS, [0, 1, 2, 3])
-        load_scale_rows(nc.sync, w_rows, w_scales, 2)
-        load_scale_rows(nc.sync, w_rows, w_scales, 3)
-        list_a = load_list("list_a", offs)
+        w_cols, ws_cols = slice(0, PASSES * R), slice(PASSES * R, DEALT)
+        sx_cols = slice(DEALT, DEALT + J)
+        landed = tile("landed", [P, DEALT + J], U8)
         w_raw = load_words("w_raw", w_words)
+        for q in range(4):
+            load_scale_rows(landed[:, w_cols], w_scales, q)
         ws_raw = load_words("ws_raw", ws_words)
         sx_codes = load_words("sx_codes", sx_words)
-        load_scale_rows(nc.sync, ws_rows, ws_scales, 0)
+        xb_planes = load_rows("xb0", xb, 0, [0, 1, 2, 3])
+        for q in range(4):
+            load_scale_rows(landed[:, ws_cols], ws_scales, q)
+        list_b = load_list("list_b", offs2)
         wb_raw = tile("wb_raw", [P, PACK * N], F32)
         nc.sync.dma_start(out=wb_raw[:], in_=wb.rearrange("(p i) n -> p (i n)", i=PACK))
-        for q in range(1, 4):
-            load_scale_rows(nc.sync, ws_rows, ws_scales, q)
-        xa_planes = load_rows("xa0", xa, 0, [0, 1])
+        for q in range(4):
+            load_scale_rows(landed[:, sx_cols], sx_scales, q)
+        xb_planes = xb_planes + load_rows("xb1", xb, K_PASS, [0, 1, 2, 3])
+        list_a = load_list("list_a", offs)
+        rw_cols = tile("rw_cols", [P, 2], F32)
+        nc.sync.dma_start(out=rw_cols[:], in_=rw.rearrange("o (p e) -> (o p) e", e=2))
+        xa_planes = load_rows("xa0", xa, 0, [0, 1, 2, 3])
         list_z = load_list("list_z", offs3)
-        for name, first_row, slots in (
-            ("xa1", 0, [2, 3]), ("xa2", K_PASS, [0, 1]), ("xa3", K_PASS, [2]), ("xa4", K_PASS, [3])
-        ):
-            xa_planes = xa_planes + load_rows(name, xa, first_row, slots)
+        for name, slots in (("xa1", [0, 1]), ("xa2", [2]), ("xa3", [3])):
+            xa_planes = xa_planes + load_rows(name, xa, K_PASS, slots)
         tz_planes = [load_rows("tz%d" % t, tz, 0, [t])[0] for t in range(PACK)]
 
-        sx_scale = tile("sx_scale", [P, J], U8)
-        nc.gpsimd.memset(sx_scale[:].bitcast(I32), 0)
-        for q in range(4):
-            load_scale_rows(nc.gpsimd, sx_scale, sx_scales, q)
-        rw_cols = tile("rw_cols", [P, 2], F32)
-        nc.gpsimd.dma_start(out=rw_cols[:], in_=rw.rearrange("o (p e) -> (o p) e", e=2))
-
-        filled = tile("filled", [P, (PASSES + 1) * R], U8)
+        filled = tile("filled", [P, DEALT + J], U8)
         nc.vector.memset(filled[:].bitcast(I32), 0)
 
         identity = tile("identity", [P, P], F32)
@@ -134,15 +129,13 @@ def tile_list_joined_rival_floored_pl_kernel(
                 nc.vector.tensor_copy(out=slots[:, :, t], in_=planes[PACK * z + t].indirect(offsets[:]))
             return quantise("u%d%d" % (h, z), grouped, E4M3)
 
-        u_b = [gather_pass(1, z, xb_planes, list_b) for z in range(PASSES)]
-
-        w_codes = deal("w_codes", w_raw, U32)
-        ws_codes = deal("ws_codes", ws_raw, U32)
+        w_codes = deal("w_codes", w_raw[:], U32, "p z m t")
+        ws_codes = deal("ws_codes", ws_raw[:], U32, "p z m t")
         for q in range(4):
             live = slice(32 * q, 32 * q + 4)
             nc.vector.tensor_copy(out=filled[live, :].bitcast(I32), in_=landed[live, :].bitcast(I32))
-        dealt_scales = deal("dealt_scales", filled, U8)
-        w_scale, ws_scale = dealt_scales[:, : PASSES * R], dealt_scales[:, PASSES * R :]
+        dealt_scales = deal("dealt_scales", filled[:, :DEALT], U8, "p z t m")
+        w_scale, ws_scale, sx_scale = dealt_scales[:, w_cols], dealt_scales[:, ws_cols], filled[:, sx_cols]
 
         def own_product(h):
             bank = psum.tile([P, PACK, HALF], F32, name="b2_bank%d" % h)
@@ -184,50 +177,53 @@ def tile_list_joined_rival_floored_pl_kernel(
             )
             return quantise("hid%d" % h, grouped, E5M2)
 
-        def second_product(h, hid):
+        def second_product(hid, pairs):
             codes, scales = hid
-            bank = psum.tile([P, PACK, HALF], F32, name="p_bank%d" % h)
             for t in range(PACK):
                 rows = slice(t * P, (t + 1) * P)
                 nc.tensor.matmul_mx(
-                    out=bank[:, t, :], lhsT=wb_codes[:, rows].bitcast(E4M3), lhsT_scale=wb_scale[:, rows],
+                    out=pairs[t // PAIR][:, t % PAIR, :], lhsT=wb_codes[:, rows].bitcast(E4M3), lhsT_scale=wb_scale[:, rows],
                     rhs=codes[:].bitcast(E5M2), rhs_scale=scales[:], start=True, stop=True,
                 )
-            return bank
 
+        wb_codes, wb_scale = quantise("wb", wb_grouped, E4M3)
         a_bank_b = psum.tile([P, PACK, HALF], F32, name="a_bank1")
         for z in range(PASSES):
-            first_pass(a_bank_b, z, u_b[z])
+            first_pass(a_bank_b, z, gather_pass(1, z, xb_planes, list_b))
         hid_b = hidden(1, a_bank_b, b2_b)
-        wb_codes, wb_scale = quantise("wb", wb_grouped, E4M3)
-        p_b = second_product(1, hid_b)
+        p_bank_b = psum.tile([P, PACK, HALF], F32, name="p_bank1")
+        p_b = [p_bank_b[:, :PAIR, :], p_bank_b[:, PAIR:, :]]
+        second_product(hid_b, p_b)
 
         a_bank_a = psum.tile([P, PACK, HALF], F32, name="a_bank0")
         for z in range(PASSES):
             first_pass(a_bank_a, z, gather_pass(0, z, xa_planes, list_a))
         hid_a = hidden(0, a_bank_a, b2_a)
-        p_a = second_product(0, hid_a)
+        p_a = [psum.tile([P, PAIR, HALF], F32, name="p_bank0%d" % u)[:] for u in range(2)]
+        second_product(hid_a, p_a)
 
-        floors = [tile("floor%d" % h, [P, PACK, HALF], F32) for h in range(2)]
+        floors = [[tile("floor%d%d" % (h, u), [P, PAIR, HALF], F32) for u in range(2)] for h in range(2)]
         for t in range(PACK):
             for h in (1, 0):
                 offsets = list_z[:, h * HALF // 16 : (h + 1) * HALF // 16]
-                nc.scalar.activation(out=floors[h][:, t, :], in_=tz_planes[t].indirect(offsets), func=COPY)
+                nc.scalar.activation(out=floors[h][t // PAIR][:, t % PAIR, :], in_=tz_planes[t].indirect(offsets), func=COPY)
 
         y_codes = tile("y_codes", [P, J], U32)
         y_scales = tile("y_scales", [P, J], U8)
         out_rows = out_0.rearrange("(p t) j -> p t j", t=PACK)
         out_words = out_1.rearrange("z p c t -> p (z c t)").bitcast(I32)
 
-        def finish(h, bank, round_on):
+        def finish(h, pairs, round_on):
             cols = slice(h * HALF, (h + 1) * HALF)
-            floored = tile("floored%d" % h, [P, PACK, HALF], F32)
-            nc.vector.tensor_tensor(out=floored[:], in0=bank[:], in1=floors[h][:], op=MAX)
+            weights = rw_rows[:, cols].unsqueeze(1).to_broadcast([P, PAIR, HALF])
+            floored = [tile("floored%d%d" % (h, u), [P, PAIR, HALF], F32) for u in range(2)]
             y = tile("y%d" % h, [P, PACK, HALF], F32)
-            nc.vector.tensor_tensor(
-                out=y[:], in0=floored[:], in1=rw_rows[:, cols].unsqueeze(1).to_broadcast([P, PACK, HALF]), op=MULT
-            )
-            nc.sync.dma_start(out=out_rows[:, :, cols], in_=y[:])
+            for u in range(2):
+                nc.vector.tensor_tensor(out=floored[u][:], in0=pairs[u], in1=floors[h][u][:], op=MAX)
+            for u in range(2):
+                slots = slice(u * PAIR, (u + 1) * PAIR)
+                nc.vector.tensor_tensor(out=y[:, slots, :], in0=floored[u][:], in1=weights, op=MULT)
+                nc.sync.dma_start(out=out_rows[:, slots, cols], in_=y[:, slots, :])
             grouped = tile("y_grouped%d" % h, [P, HALF * PACK], BF16)
             round_on(
                 out=grouped[:].rearrange("p (c i t) -> p c t i", t=PACK, i=4),

from contextlib import ExitStack

import concourse.mybir as mybir
from concourse.masks import make_identity

F32 = mybir.dt.float32
BF16 = mybir.dt.bfloat16
I32 = mybir.dt.int32
U32 = mybir.dt.uint32
U16 = mybir.dt.uint16
U8 = mybir.dt.uint8
E4M3 = mybir.dt.float8_e4m3fn_x4
E5M2 = mybir.dt.float8_e5m2_x4
MAX = mybir.AluOpType.max
MULT = mybir.AluOpType.mult
COPY = mybir.ActivationFunctionType.Copy

P = 128
PACK = 4
K_PASS = P * PACK
K, T, S, J, R, X, N, Z = 1024, 1024, 512, 256, 512, 512, 512, 512
HALF = J // 2
PASSES = K // K_PASS
PAIR = 2
DEALT = (PASSES + 1) * R

FLOPS = 2 * J * (K * R + X * R + R * N)


def tile_list_joined_rival_floored_pl_kernel(
    tc, xa, xb, w_words, w_scales, sx_words, sx_scales, ws_words, ws_scales, wb, tz, rw,
    offs, offs2, offs3, out_0, out_1, out_2,
):
    nc = tc.nc
    with ExitStack() as ctx:
        lists = ctx.enter_context(tc.tile_pool(name="lists", bufs=1))
        sb = ctx.enter_context(tc.tile_pool(name="sb", bufs=1))
        psum = ctx.enter_context(tc.psum_pool(name="psum", bufs=1))

        def tile(name, shape, dtype):
            return sb.tile(shape, dtype, name=name, align_bytes=64)

        def load_rows(name, table, first_row, slots):
            width = table.shape[1]
            rows = table[first_row : first_row + K_PASS, :].rearrange("(p t) c -> p t c", t=PACK)
            held = tile(name, [P, len(slots) * width], F32)
            nc.sync.dma_start(
                out=held[:].rearrange("p (t c) -> p t c", c=width), in_=rows[:, slots[0] : slots[-1] + 1, :]
            )
            return [held[:, i * width : (i + 1) * width] for i in range(len(slots))]

        def load_list(name, source):
            held = lists.tile(list(source.shape), U16, name=name)
            nc.sync.dma_start(held[:], source)
            return held

        def load_words(name, words):
            passes, width = words.shape[0], words.shape[2]
            held = tile(name, [P, passes * width], U32)
            nc.sync.dma_start(
                out=held[:].bitcast(I32).rearrange("p (z c) -> p z c", z=passes),
                in_=words.rearrange("z p c t -> p z (c t)").bitcast(I32),
            )
            return held

        def load_scale_rows(held, scales, q):
            nc.sync.dma_start(
                out=held[32 * q : 32 * q + 4, :].bitcast(I32).rearrange("p (z c) -> p z c", z=scales.shape[0]),
                in_=scales[:, 4 * q : 4 * q + 4, :].rearrange("z r c -> r z c").bitcast(I32),
            )

        def deal(name, held, dtype, walk):
            passes = held.shape[1] // R
            dealt = tile(name, [P, passes * R], dtype)
            nc.vector.tensor_copy(
                out=dealt[:].rearrange("p (z t m) -> " + walk, t=PACK, m=P),
                in_=held.rearrange("p (z m t) -> " + walk, t=PACK, m=P),
            )
            return dealt

        def quantise(name, grouped, fmt):
            width = grouped.shape[1] // PACK
            codes = tile(name + "_codes", [P, width], U32)
            scales = tile(name + "_scales", [P, width], U8)
            nc.vector.quantize_mx(out=codes[:].bitcast(fmt), scales=scales[:], in_=grouped[:])
            return codes, scales

        w_cols, ws_cols = slice(0, PASSES * R), slice(PASSES * R, DEALT)
        sx_cols = slice(DEALT, DEALT + J)
        landed = tile("landed", [P, DEALT + J], U8)
        w_raw = load_words("w_raw", w_words)
        for q in range(4):
            load_scale_rows(landed[:, w_cols], w_scales, q)
        ws_raw = load_words("ws_raw", ws_words)
        sx_codes = load_words("sx_codes", sx_words)
        xb_planes = load_rows("xb0", xb, 0, [0, 1, 2, 3])
        for q in range(4):
            load_scale_rows(landed[:, ws_cols], ws_scales, q)
        list_b = load_list("list_b", offs2)
        wb_raw = tile("wb_raw", [P, PACK * N], F32)
        nc.sync.dma_start(out=wb_raw[:], in_=wb.rearrange("(p i) n -> p (i n)", i=PACK))
        for q in range(4):
            load_scale_rows(landed[:, sx_cols], sx_scales, q)
        xb_planes = xb_planes + load_rows("xb1", xb, K_PASS, [0, 1, 2, 3])
        list_a = load_list("list_a", offs)
        rw_cols = tile("rw_cols", [P, 2], F32)
        nc.sync.dma_start(out=rw_cols[:], in_=rw.rearrange("o (p e) -> (o p) e", e=2))
        xa_planes = load_rows("xa0", xa, 0, [0, 1, 2, 3])
        list_z = load_list("list_z", offs3)
        for name, slots in (("xa1", [0, 1]), ("xa2", [2]), ("xa3", [3])):
            xa_planes = xa_planes + load_rows(name, xa, K_PASS, slots)
        tz_planes = [load_rows("tz%d" % t, tz, 0, [t])[0] for t in range(PACK)]

        filled = tile("filled", [P, DEALT + J], U8)
        nc.vector.memset(filled[:].bitcast(I32), 0)

        identity = tile("identity", [P, P], F32)
        make_identity(nc, identity[:])
        rw_bank = psum.tile([P, 2, P], F32, name="rw_bank")
        for e in range(2):
            nc.tensor.transpose(rw_bank[:, e, :], rw_cols[:, e : e + 1].to_broadcast([P, P]), identity[:])
        rw_rows = tile("rw_rows", [P, J], F32)
        nc.scalar.copy(out=rw_rows[:].rearrange("p (n e) -> p n e", e=2), in_=rw_bank[:].rearrange("p e n -> p n e"))

        def gather_pass(h, z, planes, offsets):
            grouped = tile("u%d%d" % (h, z), [P, HALF * PACK], BF16)
            slots = grouped[:].rearrange("p (j t) -> p j t", t=PACK)
            for t in range(PACK):
                nc.vector.tensor_copy(out=slots[:, :, t], in_=planes[PACK * z + t].indirect(offsets[:]))
            return quantise("u%d%d" % (h, z), grouped, E4M3)

        w_codes = deal("w_codes", w_raw[:], U32, "p z m t")
        ws_codes = deal("ws_codes", ws_raw[:], U32, "p z m t")
        for q in range(4):
            live = slice(32 * q, 32 * q + 4)
            nc.vector.tensor_copy(out=filled[live, :].bitcast(I32), in_=landed[live, :].bitcast(I32))
        dealt_scales = deal("dealt_scales", filled[:, :DEALT], U8, "p z t m")
        w_scale, ws_scale, sx_scale = dealt_scales[:, w_cols], dealt_scales[:, ws_cols], filled[:, sx_cols]

        def own_product(h):
            bank = psum.tile([P, PACK, HALF], F32, name="b2_bank%d" % h)
            cols = slice(h * HALF, (h + 1) * HALF)
            for t in range(PACK):
                rows = slice(t * P, (t + 1) * P)
                nc.tensor.matmul_mx(
                    out=bank[:, t, :], lhsT=ws_codes[:, rows].bitcast(E4M3), lhsT_scale=ws_scale[:, rows],
                    rhs=sx_codes[:, cols].bitcast(E4M3), rhs_scale=sx_scale[:, cols], start=True, stop=True,
                )
            b2 = tile("b2_%d" % h, [P, HALF, PACK], F32)
            nc.scalar.copy(out=b2[:], in_=bank[:].rearrange("p t j -> p j t"))
            return b2

        b2_b = own_product(1)
        b2_a = own_product(0)

        wb_grouped = tile("wb_grouped", [P, N * PACK], BF16)
        nc.scalar.copy(
            out=wb_grouped[:].rearrange("p (t m i) -> p m t i", t=PACK, i=PACK),
            in_=wb_raw[:].rearrange("p (i m t) -> p m t i", t=PACK, i=PACK),
        )

        def first_pass(bank, z, u):
            codes, scales = u
            for t in range(PACK):
                rows = slice(z * R + t * P, z * R + (t + 1) * P)
                nc.tensor.matmul_mx(
                    out=bank[:, t, :], lhsT=w_codes[:, rows].bitcast(E5M2), lhsT_scale=w_scale[:, rows],
                    rhs=codes[:].bitcast(E4M3), rhs_scale=scales[:],
                    start=(z == 0 and t == 0), stop=(z == PASSES - 1 and t == PACK - 1),
                )

        def hidden(h, bank, b2):
            grouped = tile("hid%d" % h, [P, HALF * PACK], BF16)
            nc.vector.tensor_tensor(
                out=grouped[:].rearrange("p (j t) -> p j t", t=PACK), in0=bank[:].rearrange("p t j -> p j t"),
                in1=b2[:], op=MAX,
            )
            return quantise("hid%d" % h, grouped, E5M2)

        def second_product(hid, pairs):
            codes, scales = hid
            for t in range(PACK):
                rows = slice(t * P, (t + 1) * P)
                nc.tensor.matmul_mx(
                    out=pairs[t // PAIR][:, t % PAIR, :], lhsT=wb_codes[:, rows].bitcast(E4M3), lhsT_scale=wb_scale[:, rows],
                    rhs=codes[:].bitcast(E5M2), rhs_scale=scales[:], start=True, stop=True,
                )

        wb_codes, wb_scale = quantise("wb", wb_grouped, E4M3)
        a_bank_b = psum.tile([P, PACK, HALF], F32, name="a_bank1")
        for z in range(PASSES):
            first_pass(a_bank_b, z, gather_pass(1, z, xb_planes, list_b))
        hid_b = hidden(1, a_bank_b, b2_b)
        p_bank_b = psum.tile([P, PACK, HALF], F32, name="p_bank1")
        p_b = [p_bank_b[:, :PAIR, :], p_bank_b[:, PAIR:, :]]
        second_product(hid_b, p_b)

        a_bank_a = psum.tile([P, PACK, HALF], F32, name="a_bank0")
        for z in range(PASSES):
            first_pass(a_bank_a, z, gather_pass(0, z, xa_planes, list_a))
        hid_a = hidden(0, a_bank_a, b2_a)
        p_a = [psum.tile([P, PAIR, HALF], F32, name="p_bank0%d" % u)[:] for u in range(2)]
        second_product(hid_a, p_a)

        floors = [[tile("floor%d%d" % (h, u), [P, PAIR, HALF], F32) for u in range(2)] for h in range(2)]
        for t in range(PACK):
            for h in (1, 0):
                offsets = list_z[:, h * HALF // 16 : (h + 1) * HALF // 16]
                nc.scalar.activation(out=floors[h][t // PAIR][:, t % PAIR, :], in_=tz_planes[t].indirect(offsets), func=COPY)

        y_codes = tile("y_codes", [P, J], U32)
        y_scales = tile("y_scales", [P, J], U8)
        out_rows = out_0.rearrange("(p t) j -> p t j", t=PACK)
        out_words = out_1.rearrange("z p c t -> p (z c t)").bitcast(I32)

        def finish(h, pairs, round_on):
            cols = slice(h * HALF, (h + 1) * HALF)
            weights = rw_rows[:, cols].unsqueeze(1).to_broadcast([P, PAIR, HALF])
            floored = [tile("floored%d%d" % (h, u), [P, PAIR, HALF], F32) for u in range(2)]
            y = tile("y%d" % h, [P, PACK, HALF], F32)
            for u in range(2):
                nc.vector.tensor_tensor(out=floored[u][:], in0=pairs[u], in1=floors[h][u][:], op=MAX)
            for u in range(2):
                slots = slice(u * PAIR, (u + 1) * PAIR)
                nc.vector.tensor_tensor(out=y[:, slots, :], in0=floored[u][:], in1=weights, op=MULT)
                nc.sync.dma_start(out=out_rows[:, slots, cols], in_=y[:, slots, :])
            grouped = tile("y_grouped%d" % h, [P, HALF * PACK], BF16)
            round_on(
                out=grouped[:].rearrange("p (c i t) -> p c t i", t=PACK, i=4),
                in_=y[:].rearrange("p t (c i) -> p c t i", i=4),
            )
            nc.vector.quantize_mx(out=y_codes[:, cols].bitcast(E4M3), scales=y_scales[:, cols], in_=grouped[:])
            nc.sync.dma_start(out=out_words[:, cols], in_=y_codes[:, cols].bitcast(I32))

        finish(1, p_b, nc.scalar.copy)
        finish(0, p_a, nc.vector.tensor_copy)
        for q in range(4):
            queue = nc.scalar if q % 2 else nc.sync
            queue.dma_start(
                out=out_2[0, 4 * q : 4 * q + 4, :].bitcast(I32), in_=y_scales[32 * q : 32 * q + 4, :].bitcast(I32)
            )
